import numpy as np
import ml_dtypes


def mxq(x, axis, fmt="e4m3"):
    dtype, down = {"e4m3": (ml_dtypes.float8_e4m3fn, 7), "e5m2": (ml_dtypes.float8_e5m2, 14)}[fmt]
    v = np.moveaxis(np.asarray(x, np.float32).astype(ml_dtypes.bfloat16).astype(np.float64), axis, -1)
    blocks = v.reshape(v.shape[:-1] + (-1, 32))
    amax = np.abs(blocks).max(-1, keepdims=True)
    byte = np.maximum(np.where(amax > 0, np.frexp(amax)[1] - 1 + 127, 0) - down, 1)
    scale = np.exp2(byte - 127.0)
    codes = (blocks / scale).astype(np.float32).astype(dtype).astype(np.float64)
    return np.moveaxis((codes * scale).reshape(v.shape), -1, axis)


WIDE = False


def mx_kscale(k):
    if not WIDE:
        return np.ones(k)
    levels = np.array([10, -10, 5, -5, 0])
    if k % 512:
        return np.exp2(np.random.permutation(np.resize(levels, k // 32))).repeat(32)
    a = np.empty((k // 512, 16))
    for p in range(k // 512):
        a[p, :8] = np.random.permutation(np.resize(levels, 8))
        for g in range(8):
            far = levels[np.abs(levels - a[p, g]) >= 10]
            a[p, g + 8] = far[np.random.randint(len(far))]
    return np.exp2(a.ravel()).repeat(32)


BF16 = ml_dtypes.bfloat16


def bf(x):
    return np.asarray(x, np.float32).astype(BF16)


def f64(x):
    return np.asarray(x).astype(np.float64)


E2M1 = np.array([0.0, 0.5, 1.0, 1.5, 2.0, 3.0, 4.0, 6.0, -0.0, -0.5, -1.0, -1.5, -2.0, -3.0, -4.0, -6.0])


def pack_weight(w, fmt):
    k, n = w.shape
    w = f64(bf(w)).reshape(k // 32, 32, n)
    amax = np.abs(w).max(1)
    if fmt == "e4m3":
        byte = np.frexp(amax)[1] - 1 + 127 - 7
    else:
        mant, ex = np.frexp(amax / 6.0)
        byte = np.where(mant > 0.5, ex, ex - 1) + 127
    byte = np.clip(np.where(amax > 0, byte, 1), 1, 254)
    scaled = (w * np.exp2(127.0 - byte)[:, None, :]).reshape(k, n).astype(np.float32)
    by_word = np.ascontiguousarray(scaled.reshape(k // 512, 128, 4, n).transpose(0, 1, 3, 2))
    if fmt == "e4m3":
        words = by_word.astype(ml_dtypes.float8_e4m3fn).view(np.uint8)
    else:
        c = by_word.astype(ml_dtypes.float4_e2m1fn).view(np.uint8) & 0xF
        words = c[..., 0::2] | (c[..., 1::2] << 4)
    return np.ascontiguousarray(words), np.ascontiguousarray(byte.astype(np.uint8).reshape(k // 512, 16, n))


def unpack_weight(words, scales, fmt):
    g, p, n, _ = words.shape
    if fmt == "e4m3":
        vals = np.ascontiguousarray(words).view(ml_dtypes.float8_e4m3fn).astype(np.float64)
    else:
        nib = np.empty((g, p, n, 4), np.uint8)
        nib[..., 0::2] = words & 0xF
        nib[..., 1::2] = words >> 4
        vals = E2M1[nib]
    vals = vals * np.repeat(np.exp2(scales.astype(np.float64) - 127.0), 8, axis=1)[..., None]
    return vals.transpose(0, 1, 3, 2).reshape(g * 512, n)

E4M3FN = np.array([(-1.0 if i & 128 else 1.0) * ((1.0 + (i & 7) / 8.0) * 2.0 ** (((i >> 3) & 15) - 7) if i & 120 else (i & 7) * 2.0 ** -9) for i in range(256)])


def e4m3fn_bytes(y):
    return np.clip(np.asarray(y, np.float64), -448.0, 448.0).astype(np.float32).astype(ml_dtypes.float8_e4m3fn).view(np.uint8)


def e4m3fn_values(b):
    return E4M3FN[b]


B, N, P = 1024, 1024, 512


def smoothed_root_sign(e):
    return e / np.power(e * e + 0.01, 0.25)


def smoothed_sign(e):
    return e / np.sqrt(e * e + 0.01)


def draw0():
    s, t = mx_kscale(N), mx_kscale(P)
    xh = bf(np.random.standard_normal((B, N)) * s)
    y = bf(np.random.standard_normal((B, P)) * 0.4)
    c_words, c_scales = pack_weight(np.random.standard_normal((N, P)) * (0.4 / np.sqrt(N)) / s[:, None], "e4m3")
    a_words, a_scales = pack_weight(np.random.standard_normal((N, N)) / np.sqrt(N) / s[:, None], "e4m3")
    v = bf(np.random.standard_normal((B, P)) * 0.5)
    k = bf((1.0 + 0.1 * np.random.standard_normal(P)) * t)
    l_words, l_scales = pack_weight(np.random.standard_normal((P, N)) / np.sqrt(P) / t[:, None], "e4m3")
    return {
        "xh": xh,
        "y": y,
        "c_words": c_words,
        "c_scales": c_scales,
        "a_words": a_words,
        "a_scales": a_scales,
        "v": v,
        "k": k,
        "l_words": l_words,
        "l_scales": l_scales,
    }


def core(xh, y, c_words, c_scales, a_words, a_scales, v, k, l_words, l_scales):
    vf = f64(v)
    xq = mxq(f64(xh), 1, "e4m3")
    e = f64(y) - (xq @ unpack_weight(c_words, c_scales, "e4m3"))
    m = smoothed_root_sign(e)
    j = f64(k)[None, :] * (m + vf)
    xnew = (xq @ unpack_weight(a_words, a_scales, "e4m3")) + (mxq(j, 1, "e4m3") @ unpack_weight(l_words, l_scales, "e4m3"))
    vnew = vf + 0.25 * smoothed_sign(e)
    return xnew, vnew


def setup_inputs():
    drawn = draw0()
    full = np.asarray(drawn['xh']).astype(np.float64)
    scale = (np.abs(full).reshape(8, 128, 8, 128).max(axis=(1, 3)) / 448.0).astype(np.float32)
    given = {}
    for key, value in drawn.items():
        if key == 'xh':
            given['xh_bytes'] = e4m3fn_bytes(full / np.repeat(np.repeat(scale.astype(np.float64), 128, axis=0), 128, axis=1))
            given['xh_scale'] = scale
        else:
            given[key] = value
    return given


def reference(xh_bytes, xh_scale, y, c_words, c_scales, a_words, a_scales, v, k, l_words, l_scales):
    return core(e4m3fn_values(xh_bytes) * np.repeat(np.repeat(xh_scale.astype(np.float64), 128, axis=0), 128, axis=1), y, c_words, c_scales, a_words, a_scales, v, k, l_words, l_scales)

@@ -1,0 +1,297 @@
+from contextlib import ExitStack
+
+import concourse.mybir as mybir
+from concourse.masks import make_identity
+
+B, N, P = 1024, 1024, 512
+FLOPS = 2 * B * (N * P + N * N + P * N)
+
+F32 = mybir.dt.float32
+BF16 = mybir.dt.bfloat16
+I32 = mybir.dt.int32
+U32 = mybir.dt.uint32
+U8 = mybir.dt.uint8
+FP8 = mybir.dt.float8_e4m3fn
+FP8X4 = mybir.dt.float8_e4m3fn_x4
+ALU = mybir.AluOpType
+ACT = mybir.ActivationFunctionType
+
+LANES = 128
+TILES = B // LANES
+BANK = 512
+KBLOCKS = N // LANES
+WIDEN_ON_SCALAR = 4
+
+
+def tile_smoothedsupertwistingobserverstep_d2p_kernel(
+    tc, xh_bytes, xh_scale, y, c_words, c_scales, a_words, a_scales, v, k, l_words, l_scales, out_0, out_1
+):
+    nc = tc.nc
+    with ExitStack() as ctx:
+        keep = ctx.enter_context(tc.tile_pool(name="keep", bufs=1))
+        work = ctx.enter_context(tc.tile_pool(name="work", bufs=3))
+        psum = ctx.enter_context(tc.psum_pool(name="psum", bufs=1))
+        ctx.enter_context(tc.manual_schedule())
+
+        def weight_tiles(name, words):
+            passes, width = words.shape[0], words.shape[2]
+            codes = [keep.tile([LANES, width], U32, name="%s_codes%d" % (name, g), align_bytes=64) for g in range(passes)]
+            plane = keep.tile([LANES, passes * width], U8, name=name + "_plane", align_bytes=64)
+            nc.vector.memset(plane[:].bitcast(I32), 0)
+            return codes, plane
+
+        def load_plane(plane, scales):
+            passes = scales.shape[0]
+            for r in range(4):
+                nc.sync.dma_start(
+                    out=plane[r:LANES:32, :].bitcast(I32).rearrange("q (g n) -> q g n", g=passes),
+                    in_=scales[:, r:16:4, :].bitcast(I32).rearrange("g q n -> q g n"),
+                )
+
+        def load_codes(codes, words, g):
+            nc.sync.dma_start(out=codes[g][:].bitcast(I32), in_=words[g].rearrange("p n t -> p (n t)").bitcast(I32))
+
+        def load_rows(name, src, dtype, first, count, into):
+            width = src.shape[1]
+            rows = keep.tile([LANES, count * width], dtype, name="%s%d" % (name, first), align_bytes=64)
+            nc.sync.dma_start(
+                out=rows[:].rearrange("p (i w) -> p i w", i=count),
+                in_=src[first * LANES : (first + count) * LANES, :].rearrange("(i p) w -> p i w", p=LANES),
+            )
+            into.extend([rows[:, i * width : (i + 1) * width] for i in range(count)])
+
+        c_codes, c_plane = weight_tiles("c", c_words)
+        l_codes, l_plane = weight_tiles("l", l_words)
+        a_codes, a_plane = weight_tiles("a", a_words)
+        ident = keep.tile([LANES, LANES], F32)
+        make_identity(nc, ident[:])
+        ident_bf16 = keep.tile([LANES, LANES], BF16)
+        make_identity(nc, ident_bf16[:])
+
+        xb, yb, vb = [], [], []
+        xscale = keep.tile([LANES, TILES * KBLOCKS], F32)
+        gain = keep.tile([LANES, 4], BF16)
+        nc.sync.dma_start(out=xscale[:], in_=xh_scale.rearrange("i j -> (i j)").partition_broadcast(LANES))
+        load_rows("xbytes", xh_bytes, U8, 0, 1, xb)
+        load_rows("xbytes", xh_bytes, U8, 1, 1, xb)
+        load_plane(c_plane, c_scales)
+        load_codes(c_codes, c_words, 0)
+        load_codes(c_codes, c_words, 1)
+        load_rows("xbytes", xh_bytes, U8, 2, 2, xb)
+        load_rows("yrows", y, BF16, 0, 2, yb)
+        load_rows("xbytes", xh_bytes, U8, 4, 4, xb)
+        load_rows("vrows", v, BF16, 0, 2, vb)
+        load_rows("yrows", y, BF16, 2, 2, yb)
+        nc.sync.dma_start(out=gain[:], in_=k.rearrange("(p t) -> p t", t=4))
+        load_plane(a_plane, a_scales)
+        load_plane(l_plane, l_scales)
+        load_codes(a_codes, a_words, 0)
+        load_codes(a_codes, a_words, 1)
+        load_codes(l_codes, l_words, 0)
+        load_rows("vrows", v, BF16, 2, 2, vb)
+        load_rows("yrows", y, BF16, 4, 4, yb)
+        load_rows("vrows", v, BF16, 4, 4, vb)
+
+        held = {}
+
+        def mx(out, left, left_cols, codes, plane, start, stop):
+            left_codes, left_plane = left
+            nc.tensor.matmul_mx(
+                out=out,
+                lhsT=left_codes[:, left_cols].bitcast(FP8X4),
+                lhsT_scale=left_plane[:, left_cols],
+                rhs=codes.bitcast(FP8X4),
+                rhs_scale=plane,
+                start=start,
+                stop=stop,
+            )
+
+        def widen_block(i, j):
+            if ("wide", i) not in held:
+                held["wide", i] = work.tile([LANES, N], BF16, name="wide", bufs=4, align_bytes=64)
+            cols = slice(j * LANES, (j + 1) * LANES)
+            factor = xscale[:, i * KBLOCKS + j : i * KBLOCKS + j + 1]
+            return held["wide", i][:, cols], xb[i][:, cols].bitcast(FP8), factor
+
+        def widen_on_vector(i):
+            for j in range(KBLOCKS - WIDEN_ON_SCALAR):
+                wide, raw, factor = widen_block(i, j)
+                nc.vector.tensor_scalar(out=wide, in0=raw, scalar1=factor, scalar2=None, op0=ALU.mult)
+
+        def widen_on_scalar(i):
+            for j in range(KBLOCKS - WIDEN_ON_SCALAR, KBLOCKS):
+                wide, raw, factor = widen_block(i, j)
+                nc.scalar.activation(out=wide, in_=raw, func=ACT.Copy, scale=factor)
+
+        def turn_x(i):
+            words = held["wide", i][:].bitcast(F32)
+            turned = psum.tile([LANES, 4, LANES], F32, bufs=2)
+            for g in range(2):
+                for u in range(2):
+                    nc.tensor.transpose(turned[:, 2 * g + u, :], words[:, 256 * g + u : 256 * (g + 1) : 2], ident[:])
+            held["turned", i] = turned
+
+        def group_x(i):
+            grouped = work.tile([LANES, N], BF16, align_bytes=64)
+            nc.scalar.copy(
+                out=grouped[:].bitcast(F32).rearrange("p (g r u) -> p g r u", g=2, u=2),
+                in_=held["turned", i][:].rearrange("p (g u) r -> p g r u", u=2),
+            )
+            held["grouped", i] = grouped
+
+        def quantise_x(i):
+            x_codes = keep.tile([LANES, 2 * LANES], U32, name="x_codes%d" % i, align_bytes=64)
+            x_plane = keep.tile([LANES, 2 * LANES], U8, name="x_plane%d" % i, align_bytes=64)
+            nc.vector.quantize_mx(out=x_codes[:].bitcast(FP8X4), scales=x_plane[:], in_=held["grouped", i][:])
+            held["xq", i] = (x_codes, x_plane)
+
+        def fit_pass(i, g):
+            if g == 0:
+                held["fit", i] = psum.tile([LANES, P], F32, name="fit", bufs=1)
+            tok = slice(g * LANES, (g + 1) * LANES)
+            mx(held["fit", i][:], held["xq", i], tok, c_codes[g][:], c_plane[:, g * P : (g + 1) * P], g == 0, g == 1)
+
+        def error(i):
+            err = work.tile([LANES, P], F32)
+            nc.vector.tensor_tensor(
+                out=err[:].rearrange("p (t b i) -> p b t i", t=4, i=4),
+                in0=yb[i].rearrange("p (b i t) -> p b t i", t=4, i=4),
+                in1=held["fit", i][:].rearrange("p (b i t) -> p b t i", t=4, i=4),
+                op=ALU.subtract,
+            )
+            held["err", i] = err
+
+        def square(i):
+            sq = work.tile([LANES, P], F32)
+            nc.scalar.activation(out=sq[:], in_=held["err", i][:], func=ACT.Square)
+            held["sq", i] = sq
+
+        def inverse_root(i):
+            inv_root = work.tile([LANES, P], F32)
+            nc.scalar.activation(out=inv_root[:], in_=held["sq", i][:], func=ACT.Abs_reciprocal_sqrt, bias=0.01)
+            held["inv_root", i] = inv_root
+
+        def fourth_root(i):
+            fourth = work.tile([LANES, P], F32)
+            nc.scalar.activation(out=fourth[:], in_=held["inv_root", i][:], func=ACT.Abs_reciprocal_sqrt)
+            held["fourth", i] = fourth
+
+        def smooth_sign(i):
+            sgn = work.tile([LANES, P], F32)
+            nc.vector.tensor_tensor(out=sgn[:], in0=held["err", i][:], in1=held["inv_root", i][:], op=ALU.mult)
+            held["sgn", i] = sgn
+
+        def root_sign(i):
+            m = work.tile([LANES, P], F32)
+            nc.vector.tensor_tensor(out=m[:], in0=held["sgn", i][:], in1=held["fourth", i][:], op=ALU.mult)
+            held["m", i] = m
+
+        def update_v(i):
+            vnew = work.tile([LANES, P], F32)
+            nc.vector.scalar_tensor_tensor(
+                out=vnew[:].rearrange("p (c t) -> p c t", t=4),
+                in0=held["sgn", i][:].rearrange("p (t c) -> p c t", t=4),
+                scalar=0.25,
+                in1=vb[i].rearrange("p (c t) -> p c t", t=4),
+                op0=ALU.mult,
+                op1=ALU.add,
+            )
+            nc.sync.dma_start(out=out_1[i * LANES : (i + 1) * LANES, :], in_=vnew[:])
+
+        def turn_v(i, t):
+            if t == 0:
+                held["sum", i] = psum.tile([LANES, 4, LANES], F32, name="turned_sum", bufs=1)
+            nc.tensor.matmul(held["sum", i][:, t, :], lhsT=vb[i][:, t:P:4], rhs=ident_bf16[:], start=(t == 0), stop=False)
+
+        def turn_m(i):
+            for t in range(4):
+                nc.tensor.matmul(
+                    held["sum", i][:, t, :],
+                    lhsT=held["m", i][:, t * LANES : (t + 1) * LANES],
+                    rhs=ident[:],
+                    is_transpose=True,
+                    start=False,
+                    stop=(t == 3),
+                )
+
+        def apply_gain(i):
+            inject = work.tile([LANES, P], BF16, align_bytes=64)
+            nc.vector.tensor_tensor(
+                out=inject[:].rearrange("p (r t) -> p r t", t=4),
+                in0=held["sum", i][:].rearrange("p t r -> p r t"),
+                in1=gain[:].unsqueeze(1).to_broadcast([LANES, LANES, 4]),
+                op=ALU.mult,
+            )
+            held["inject", i] = inject
+
+        def quantise_j(i):
+            j_codes = work.tile([LANES, LANES], U32, align_bytes=64)
+            j_plane = work.tile([LANES, LANES], U8, align_bytes=64)
+            nc.vector.quantize_mx(out=j_codes[:].bitcast(FP8X4), scales=j_plane[:], in_=held["inject", i][:])
+            held["jq", i] = (j_codes, j_plane)
+
+        def state_passes(i):
+            for h in range(2):
+                acc = psum.tile([LANES, BANK], F32, bufs=4)
+                for g in range(2):
+                    tok = slice(g * LANES, (g + 1) * LANES)
+                    codes = a_codes[g][:, h * BANK : (h + 1) * BANK]
+                    plane = a_plane[:, g * N + h * BANK : g * N + (h + 1) * BANK]
+                    mx(acc[:], held["xq", i], tok, codes, plane, g == 0, False)
+                held["acc", i, h] = acc
+
+        def inject_pass(i, h):
+            cols = slice(h * BANK, (h + 1) * BANK)
+            mx(held["acc", i, h][:], held["jq", i], slice(0, LANES), l_codes[0][:, cols], l_plane[:, cols], False, True)
+
+        def store_x(i, h):
+            xnew = work.tile([LANES, BANK], F32, bufs=4)
+            if i == TILES - 1 and h == 1:
+                nc.vector.tensor_copy(out=xnew[:], in_=held["acc", i, h][:])
+            else:
+                nc.scalar.copy(out=xnew[:], in_=held["acc", i, h][:])
+            nc.sync.dma_start(out=out_0[i * LANES : (i + 1) * LANES, h * BANK : (h + 1) * BANK], in_=xnew[:])
+
+        def on(stage, i, *rest):
+            if 0 <= i < TILES:
+                stage(i, *rest)
+
+        def turned_in(s):
+            if s < 0:
+                return [s + 3] if s >= -3 else []
+            if s == 0:
+                return [3, 4]
+            return [s + 4] if s + 4 < TILES else []
+
+        for s in range(-4, TILES + 2):
+            on(root_sign, s - 1)
+            on(square, s)
+            on(fit_pass, s + 1, 0)
+            on(turn_v, s - 1, 0)
+            on(fit_pass, s + 1, 1)
+            on(turn_v, s - 1, 1)
+            on(inject_pass, s - 2, 0)
+            on(turn_v, s - 1, 2)
+            on(inject_pass, s - 2, 1)
+            on(turn_v, s - 1, 3)
+            for i in turned_in(s - 1):
+                group_x(i)
+            on(update_v, s - 1)
+            for i in turned_in(s + 1):
+                widen_on_vector(i)
+            on(inverse_root, s)
+            on(store_x, s - 2, 0)
+            on(turn_m, s - 1)
+            on(error, s + 1)
+            on(apply_gain, s - 1)
+            on(smooth_sign, s)
+            for i in turned_in(s - 1):
+                quantise_x(i)
+            on(quantise_j, s - 1)
+            on(fourth_root, s)
+            on(store_x, s - 2, 1)
+            for i in turned_in(s + 1):
+                widen_on_scalar(i)
+            for i in turned_in(s):
+                turn_x(i)
+            on(state_passes, s - 1)

@@ -35,7 +35,7 @@ def tile_smoothedsupertwistingobserverstep_d2p_kernel(
 
         def weight_tiles(name, words):
             passes, width = words.shape[0], words.shape[2]
-            codes = [keep.tile([LANES, width], U32, name="%s_codes%d" % (name, g), align_bytes=64) for g in range(passes)]
+            codes = keep.tile([LANES, passes * width], U32, name=name + "_codes", align_bytes=64)
             plane = keep.tile([LANES, passes * width], U8, name=name + "_plane", align_bytes=64)
             nc.vector.memset(plane[:].bitcast(I32), 0)
             return codes, plane
@@ -48,8 +48,11 @@ def tile_smoothedsupertwistingobserverstep_d2p_kernel(
                     in_=scales[:, r:16:4, :].bitcast(I32).rearrange("g q n -> q g n"),
                 )
 
-        def load_codes(codes, words, g):
-            nc.sync.dma_start(out=codes[g][:].bitcast(I32), in_=words[g].rearrange("p n t -> p (n t)").bitcast(I32))
+        def load_codes(codes, words):
+            nc.sync.dma_start(
+                out=codes[:].bitcast(I32).rearrange("p (g n) -> p g n", g=words.shape[0]),
+                in_=words.rearrange("g p n t -> p g (n t)").bitcast(I32),
+            )
 
         def load_rows(name, src, dtype, first, count, into):
             width = src.shape[1]
@@ -60,6 +63,9 @@ def tile_smoothedsupertwistingobserverstep_d2p_kernel(
             )
             into.extend([rows[:, i * width : (i + 1) * width] for i in range(count)])
 
+        warm = keep.tile([LANES, 2], F32)
+        nc.vector.memset(warm[:, 0:1], 1.0)
+        nc.scalar.activation(out=warm[:, 1:2], in_=warm[:, 0:1], func=ACT.Abs_reciprocal_sqrt)
         c_codes, c_plane = weight_tiles("c", c_words)
         l_codes, l_plane = weight_tiles("l", l_words)
         a_codes, a_plane = weight_tiles("a", a_words)
@@ -75,19 +81,17 @@ def tile_smoothedsupertwistingobserverstep_d2p_kernel(
         load_rows("xbytes", xh_bytes, U8, 0, 1, xb)
         load_rows("xbytes", xh_bytes, U8, 1, 1, xb)
         load_plane(c_plane, c_scales)
-        load_codes(c_codes, c_words, 0)
-        load_codes(c_codes, c_words, 1)
+        load_codes(c_codes, c_words)
         load_rows("xbytes", xh_bytes, U8, 2, 2, xb)
         load_rows("yrows", y, BF16, 0, 2, yb)
         load_rows("xbytes", xh_bytes, U8, 4, 4, xb)
-        load_rows("vrows", v, BF16, 0, 2, vb)
-        load_rows("yrows", y, BF16, 2, 2, yb)
-        nc.sync.dma_start(out=gain[:], in_=k.rearrange("(p t) -> p t", t=4))
         load_plane(a_plane, a_scales)
         load_plane(l_plane, l_scales)
-        load_codes(a_codes, a_words, 0)
-        load_codes(a_codes, a_words, 1)
-        load_codes(l_codes, l_words, 0)
+        nc.sync.dma_start(out=gain[:], in_=k.rearrange("(p t) -> p t", t=4))
+        load_rows("vrows", v, BF16, 0, 2, vb)
+        load_rows("yrows", y, BF16, 2, 2, yb)
+        load_codes(a_codes, a_words)
+        load_codes(l_codes, l_words)
         load_rows("vrows", v, BF16, 2, 2, vb)
         load_rows("yrows", y, BF16, 4, 4, yb)
         load_rows("vrows", v, BF16, 4, 4, vb)
@@ -149,7 +153,7 @@ def tile_smoothedsupertwistingobserverstep_d2p_kernel(
             if g == 0:
                 held["fit", i] = psum.tile([LANES, P], F32, name="fit", bufs=1)
             tok = slice(g * LANES, (g + 1) * LANES)
-            mx(held["fit", i][:], held["xq", i], tok, c_codes[g][:], c_plane[:, g * P : (g + 1) * P], g == 0, g == 1)
+            mx(held["fit", i][:], held["xq", i], tok, c_codes[:, g * P : (g + 1) * P], c_plane[:, g * P : (g + 1) * P], g == 0, g == 1)
 
         def error(i):
             err = work.tile([LANES, P], F32)
@@ -168,12 +172,12 @@ def tile_smoothedsupertwistingobserverstep_d2p_kernel(
 
         def inverse_root(i):
             inv_root = work.tile([LANES, P], F32)
-            nc.scalar.activation(out=inv_root[:], in_=held["sq", i][:], func=ACT.Abs_reciprocal_sqrt, bias=0.01)
+            nc.scalar.activation(out=inv_root[:], in_=held["sq", i][:], func=ACT.Abs_reciprocal_sqrt, scale=16.0, bias=0.16)
             held["inv_root", i] = inv_root
 
         def fourth_root(i):
             fourth = work.tile([LANES, P], F32)
-            nc.scalar.activation(out=fourth[:], in_=held["inv_root", i][:], func=ACT.Abs_reciprocal_sqrt)
+            nc.scalar.activation(out=fourth[:], in_=held["inv_root", i][:], func=ACT.Abs_reciprocal_sqrt, scale=0.25)
             held["fourth", i] = fourth
 
         def smooth_sign(i):
@@ -188,13 +192,11 @@ def tile_smoothedsupertwistingobserverstep_d2p_kernel(
 
         def update_v(i):
             vnew = work.tile([LANES, P], F32)
-            nc.vector.scalar_tensor_tensor(
-                out=vnew[:].rearrange("p (c t) -> p c t", t=4),
-                in0=held["sgn", i][:].rearrange("p (t c) -> p c t", t=4),
-                scalar=0.25,
-                in1=vb[i].rearrange("p (c t) -> p c t", t=4),
-                op0=ALU.mult,
-                op1=ALU.add,
+            nc.vector.tensor_tensor(
+                out=vnew[:].rearrange("p (b i t) -> p b t i", t=4, i=4),
+                in0=held["sgn", i][:].rearrange("p (t b i) -> p b t i", t=4, i=4),
+                in1=vb[i].rearrange("p (b i t) -> p b t i", t=4, i=4),
+                op=ALU.add,
             )
             nc.sync.dma_start(out=out_1[i * LANES : (i + 1) * LANES, :], in_=vnew[:])
 
@@ -235,14 +237,14 @@ def tile_smoothedsupertwistingobserverstep_d2p_kernel(
                 acc = psum.tile([LANES, BANK], F32, bufs=4)
                 for g in range(2):
                     tok = slice(g * LANES, (g + 1) * LANES)
-                    codes = a_codes[g][:, h * BANK : (h + 1) * BANK]
+                    codes = a_codes[:, g * N + h * BANK : g * N + (h + 1) * BANK]
                     plane = a_plane[:, g * N + h * BANK : g * N + (h + 1) * BANK]
                     mx(acc[:], held["xq", i], tok, codes, plane, g == 0, False)
                 held["acc", i, h] = acc
 
         def inject_pass(i, h):
             cols = slice(h * BANK, (h + 1) * BANK)
-            mx(held["acc", i, h][:], held["jq", i], slice(0, LANES), l_codes[0][:, cols], l_plane[:, cols], False, True)
+            mx(held["acc", i, h][:], held["jq", i], slice(0, LANES), l_codes[:, cols], l_plane[:, cols], False, True)
 
         def store_x(i, h):
             xnew = work.tile([LANES, BANK], F32, bufs=4)

@@ -79,17 +79,17 @@ def tile_smoothedsupertwistingobserverstep_d2p_kernel(
         gain = keep.tile([LANES, 4], BF16)
         nc.sync.dma_start(out=xscale[:], in_=xh_scale.rearrange("i j -> (i j)").partition_broadcast(LANES))
         load_rows("xbytes", xh_bytes, U8, 0, 1, xb)
-        load_rows("xbytes", xh_bytes, U8, 1, 1, xb)
-        load_plane(c_plane, c_scales)
+        load_rows("xbytes", xh_bytes, U8, 1, 3, xb)
         load_codes(c_codes, c_words)
-        load_rows("xbytes", xh_bytes, U8, 2, 2, xb)
+        load_plane(c_plane, c_scales)
         load_rows("yrows", y, BF16, 0, 2, yb)
-        load_rows("xbytes", xh_bytes, U8, 4, 4, xb)
+        load_rows("xbytes", xh_bytes, U8, 4, 2, xb)
         load_plane(a_plane, a_scales)
         load_plane(l_plane, l_scales)
         nc.sync.dma_start(out=gain[:], in_=k.rearrange("(p t) -> p t", t=4))
         load_rows("vrows", v, BF16, 0, 2, vb)
         load_rows("yrows", y, BF16, 2, 2, yb)
+        load_rows("xbytes", xh_bytes, U8, 6, 2, xb)
         load_codes(a_codes, a_words)
         load_codes(l_codes, l_words)
         load_rows("vrows", v, BF16, 2, 2, vb)
@@ -157,12 +157,7 @@ def tile_smoothedsupertwistingobserverstep_d2p_kernel(
 
         def error(i):
             err = work.tile([LANES, P], F32)
-            nc.vector.tensor_tensor(
-                out=err[:].rearrange("p (t b i) -> p b t i", t=4, i=4),
-                in0=yb[i].rearrange("p (b i t) -> p b t i", t=4, i=4),
-                in1=held["fit", i][:].rearrange("p (b i t) -> p b t i", t=4, i=4),
-                op=ALU.subtract,
-            )
+            nc.vector.tensor_tensor(out=err[:], in0=yb[i], in1=held["fit", i][:], op=ALU.subtract)
             held["err", i] = err
 
         def square(i):
@@ -187,17 +182,17 @@ def tile_smoothedsupertwistingobserverstep_d2p_kernel(
 
         def root_sign(i):
             m = work.tile([LANES, P], F32)
-            nc.vector.tensor_tensor(out=m[:], in0=held["sgn", i][:], in1=held["fourth", i][:], op=ALU.mult)
+            nc.vector.tensor_tensor(
+                out=m[:].rearrange("p (u c e) -> p u c e", u=2, e=2),
+                in0=held["sgn", i][:].rearrange("p (c u e) -> p u c e", u=2, e=2),
+                in1=held["fourth", i][:].rearrange("p (c u e) -> p u c e", u=2, e=2),
+                op=ALU.mult,
+            )
             held["m", i] = m
 
         def update_v(i):
             vnew = work.tile([LANES, P], F32)
-            nc.vector.tensor_tensor(
-                out=vnew[:].rearrange("p (b i t) -> p b t i", t=4, i=4),
-                in0=held["sgn", i][:].rearrange("p (t b i) -> p b t i", t=4, i=4),
-                in1=vb[i].rearrange("p (b i t) -> p b t i", t=4, i=4),
-                op=ALU.add,
-            )
+            nc.vector.tensor_tensor(out=vnew[:], in0=held["sgn", i][:], in1=vb[i], op=ALU.add)
             nc.sync.dma_start(out=out_1[i * LANES : (i + 1) * LANES, :], in_=vnew[:])
 
         def turn_v(i, t):
@@ -209,7 +204,7 @@ def tile_smoothedsupertwistingobserverstep_d2p_kernel(
             for t in range(4):
                 nc.tensor.matmul(
                     held["sum", i][:, t, :],
-                    lhsT=held["m", i][:, t * LANES : (t + 1) * LANES],
+                    lhsT=held["m", i][:, 256 * (t // 2) + t % 2 : 256 * (t // 2 + 1) : 2],
                     rhs=ident[:],
                     is_transpose=True,
                     start=False,
@@ -219,9 +214,9 @@ def tile_smoothedsupertwistingobserverstep_d2p_kernel(
         def apply_gain(i):
             inject = work.tile([LANES, P], BF16, align_bytes=64)
             nc.vector.tensor_tensor(
-                out=inject[:].rearrange("p (r t) -> p r t", t=4),
-                in0=held["sum", i][:].rearrange("p t r -> p r t"),
-                in1=gain[:].unsqueeze(1).to_broadcast([LANES, LANES, 4]),
+                out=inject[:].rearrange("p (r i t) -> p r t i", i=2, t=4),
+                in0=held["sum", i][:].rearrange("p t (r i) -> p r t i", i=2),
+                in1=gain[:].unsqueeze(1).unsqueeze(3).to_broadcast([LANES, LANES // 2, 4, 2]),
                 op=ALU.mult,
             )
             held["inject", i] = inject
@@ -259,13 +254,9 @@ def tile_smoothedsupertwistingobserverstep_d2p_kernel(
                 stage(i, *rest)
 
         def turned_in(s):
-            if s < 0:
-                return [s + 3] if s >= -3 else []
-            if s == 0:
-                return [3, 4]
-            return [s + 4] if s + 4 < TILES else []
+            return [s + 4] if 0 <= s + 4 < TILES else []
 
-        for s in range(-4, TILES + 2):
+        for s in range(-5, TILES + 2):
             on(root_sign, s - 1)
             on(square, s)
             on(fit_pass, s + 1, 0)

@@ -20,7 +20,7 @@ LANES = 128
 TILES = B // LANES
 BANK = 512
 KBLOCKS = N // LANES
-WIDEN_ON_SCALAR = 4
+WIDEN_ON_SCALAR = 3
 
 
 def tile_smoothedsupertwistingobserverstep_d2p_kernel(
@@ -157,7 +157,12 @@ def tile_smoothedsupertwistingobserverstep_d2p_kernel(
 
         def error(i):
             err = work.tile([LANES, P], F32)
-            nc.vector.tensor_tensor(out=err[:], in0=yb[i], in1=held["fit", i][:], op=ALU.subtract)
+            nc.vector.tensor_tensor(
+                out=err[:].rearrange("p (u c e) -> p u c e", u=2, e=2),
+                in0=yb[i].rearrange("p (c u e) -> p u c e", u=2, e=2),
+                in1=held["fit", i][:].rearrange("p (c u e) -> p u c e", u=2, e=2),
+                op=ALU.subtract,
+            )
             held["err", i] = err
 
         def square(i):
@@ -183,16 +188,21 @@ def tile_smoothedsupertwistingobserverstep_d2p_kernel(
         def root_sign(i):
             m = work.tile([LANES, P], F32)
             nc.vector.tensor_tensor(
-                out=m[:].rearrange("p (u c e) -> p u c e", u=2, e=2),
-                in0=held["sgn", i][:].rearrange("p (c u e) -> p u c e", u=2, e=2),
-                in1=held["fourth", i][:].rearrange("p (c u e) -> p u c e", u=2, e=2),
+                out=m[:].rearrange("p (u e c) -> p u e c", u=2, e=2),
+                in0=held["sgn", i][:].rearrange("p (u c e) -> p u e c", u=2, e=2),
+                in1=held["fourth", i][:].rearrange("p (u c e) -> p u e c", u=2, e=2),
                 op=ALU.mult,
             )
             held["m", i] = m
 
         def update_v(i):
             vnew = work.tile([LANES, P], F32)
-            nc.vector.tensor_tensor(out=vnew[:], in0=held["sgn", i][:], in1=vb[i], op=ALU.add)
+            nc.vector.tensor_tensor(
+                out=vnew[:].rearrange("p (c u e) -> p c u e", u=2, e=2),
+                in0=held["sgn", i][:].rearrange("p (u c e) -> p c u e", u=2, e=2),
+                in1=vb[i].rearrange("p (c u e) -> p c u e", u=2, e=2),
+                op=ALU.add,
+            )
             nc.sync.dma_start(out=out_1[i * LANES : (i + 1) * LANES, :], in_=vnew[:])
 
         def turn_v(i, t):
@@ -204,7 +214,7 @@ def tile_smoothedsupertwistingobserverstep_d2p_kernel(
             for t in range(4):
                 nc.tensor.matmul(
                     held["sum", i][:, t, :],
-                    lhsT=held["m", i][:, 256 * (t // 2) + t % 2 : 256 * (t // 2 + 1) : 2],
+                    lhsT=held["m", i][:, t * LANES : (t + 1) * LANES],
                     rhs=ident[:],
                     is_transpose=True,
                     start=False,

from contextlib import ExitStack

import concourse.mybir as mybir
from concourse.masks import make_identity

B, N, P = 1024, 1024, 512
FLOPS = 2 * B * (N * P + N * N + P * N)

F32 = mybir.dt.float32
BF16 = mybir.dt.bfloat16
I32 = mybir.dt.int32
U32 = mybir.dt.uint32
U8 = mybir.dt.uint8
FP8 = mybir.dt.float8_e4m3fn
FP8X4 = mybir.dt.float8_e4m3fn_x4
ALU = mybir.AluOpType
ACT = mybir.ActivationFunctionType

LANES = 128
TILES = B // LANES
BANK = 512
KBLOCKS = N // LANES
WIDEN_ON_SCALAR = 3


def tile_smoothedsupertwistingobserverstep_d2p_kernel(
    tc, xh_bytes, xh_scale, y, c_words, c_scales, a_words, a_scales, v, k, l_words, l_scales, out_0, out_1
):
    nc = tc.nc
    with ExitStack() as ctx:
        keep = ctx.enter_context(tc.tile_pool(name="keep", bufs=1))
        work = ctx.enter_context(tc.tile_pool(name="work", bufs=3))
        psum = ctx.enter_context(tc.psum_pool(name="psum", bufs=1))
        ctx.enter_context(tc.manual_schedule())

        def weight_tiles(name, words):
            passes, width = words.shape[0], words.shape[2]
            codes = keep.tile([LANES, passes * width], U32, name=name + "_codes", align_bytes=64)
            plane = keep.tile([LANES, passes * width], U8, name=name + "_plane", align_bytes=64)
            nc.vector.memset(plane[:].bitcast(I32), 0)
            return codes, plane

        def load_plane(plane, scales):
            passes = scales.shape[0]
            for r in range(4):
                nc.sync.dma_start(
                    out=plane[r:LANES:32, :].bitcast(I32).rearrange("q (g n) -> q g n", g=passes),
                    in_=scales[:, r:16:4, :].bitcast(I32).rearrange("g q n -> q g n"),
                )

        def load_codes(codes, words):
            nc.sync.dma_start(
                out=codes[:].bitcast(I32).rearrange("p (g n) -> p g n", g=words.shape[0]),
                in_=words.rearrange("g p n t -> p g (n t)").bitcast(I32),
            )

        def load_rows(name, src, dtype, first, count, into):
            width = src.shape[1]
            rows = keep.tile([LANES, count * width], dtype, name="%s%d" % (name, first), align_bytes=64)
            nc.sync.dma_start(
                out=rows[:].rearrange("p (i w) -> p i w", i=count),
                in_=src[first * LANES : (first + count) * LANES, :].rearrange("(i p) w -> p i w", p=LANES),
            )
            into.extend([rows[:, i * width : (i + 1) * width] for i in range(count)])

        warm = keep.tile([LANES, 2], F32)
        nc.vector.memset(warm[:, 0:1], 1.0)
        nc.scalar.activation(out=warm[:, 1:2], in_=warm[:, 0:1], func=ACT.Abs_reciprocal_sqrt)
        c_codes, c_plane = weight_tiles("c", c_words)
        l_codes, l_plane = weight_tiles("l", l_words)
        a_codes, a_plane = weight_tiles("a", a_words)
        ident = keep.tile([LANES, LANES], F32)
        make_identity(nc, ident[:])
        ident_bf16 = keep.tile([LANES, LANES], BF16)
        make_identity(nc, ident_bf16[:])

        xb, yb, vb = [], [], []
        xscale = keep.tile([LANES, TILES * KBLOCKS], F32)
        gain = keep.tile([LANES, 4], BF16)
        nc.sync.dma_start(out=xscale[:], in_=xh_scale.rearrange("i j -> (i j)").partition_broadcast(LANES))
        load_rows("xbytes", xh_bytes, U8, 0, 1, xb)
        load_rows("xbytes", xh_bytes, U8, 1, 3, xb)
        load_codes(c_codes, c_words)
        load_plane(c_plane, c_scales)
        load_rows("yrows", y, BF16, 0, 2, yb)
        load_rows("xbytes", xh_bytes, U8, 4, 2, xb)
        load_plane(a_plane, a_scales)
        load_plane(l_plane, l_scales)
        nc.sync.dma_start(out=gain[:], in_=k.rearrange("(p t) -> p t", t=4))
        load_rows("vrows", v, BF16, 0, 2, vb)
        load_rows("yrows", y, BF16, 2, 2, yb)
        load_rows("xbytes", xh_bytes, U8, 6, 2, xb)
        load_codes(a_codes, a_words)
        load_codes(l_codes, l_words)
        load_rows("vrows", v, BF16, 2, 2, vb)
        load_rows("yrows", y, BF16, 4, 4, yb)
        load_rows("vrows", v, BF16, 4, 4, vb)

        held = {}

        def mx(out, left, left_cols, codes, plane, start, stop):
            left_codes, left_plane = left
            nc.tensor.matmul_mx(
                out=out,
                lhsT=left_codes[:, left_cols].bitcast(FP8X4),
                lhsT_scale=left_plane[:, left_cols],
                rhs=codes.bitcast(FP8X4),
                rhs_scale=plane,
                start=start,
                stop=stop,
            )

        def widen_block(i, j):
            if ("wide", i) not in held:
                held["wide", i] = work.tile([LANES, N], BF16, name="wide", bufs=4, align_bytes=64)
            cols = slice(j * LANES, (j + 1) * LANES)
            factor = xscale[:, i * KBLOCKS + j : i * KBLOCKS + j + 1]
            return held["wide", i][:, cols], xb[i][:, cols].bitcast(FP8), factor

        def widen_on_vector(i):
            for j in range(KBLOCKS - WIDEN_ON_SCALAR):
                wide, raw, factor = widen_block(i, j)
                nc.vector.tensor_scalar(out=wide, in0=raw, scalar1=factor, scalar2=None, op0=ALU.mult)

        def widen_on_scalar(i):
            for j in range(KBLOCKS - WIDEN_ON_SCALAR, KBLOCKS):
                wide, raw, factor = widen_block(i, j)
                nc.scalar.activation(out=wide, in_=raw, func=ACT.Copy, scale=factor)

        def turn_x(i):
            words = held["wide", i][:].bitcast(F32)
            turned = psum.tile([LANES, 4, LANES], F32, bufs=2)
            for g in range(2):
                for u in range(2):
                    nc.tensor.transpose(turned[:, 2 * g + u, :], words[:, 256 * g + u : 256 * (g + 1) : 2], ident[:])
            held["turned", i] = turned

        def group_x(i):
            grouped = work.tile([LANES, N], BF16, align_bytes=64)
            nc.scalar.copy(
                out=grouped[:].bitcast(F32).rearrange("p (g r u) -> p g r u", g=2, u=2),
                in_=held["turned", i][:].rearrange("p (g u) r -> p g r u", u=2),
            )
            held["grouped", i] = grouped

        def quantise_x(i):
            x_codes = keep.tile([LANES, 2 * LANES], U32, name="x_codes%d" % i, align_bytes=64)
            x_plane = keep.tile([LANES, 2 * LANES], U8, name="x_plane%d" % i, align_bytes=64)
            nc.vector.quantize_mx(out=x_codes[:].bitcast(FP8X4), scales=x_plane[:], in_=held["grouped", i][:])
            held["xq", i] = (x_codes, x_plane)

        def fit_pass(i, g):
            if g == 0:
                held["fit", i] = psum.tile([LANES, P], F32, name="fit", bufs=1)
            tok = slice(g * LANES, (g + 1) * LANES)
            mx(held["fit", i][:], held["xq", i], tok, c_codes[:, g * P : (g + 1) * P], c_plane[:, g * P : (g + 1) * P], g == 0, g == 1)

        def error(i):
            err = work.tile([LANES, P], F32)
            nc.vector.tensor_tensor(
                out=err[:].rearrange("p (u c e) -> p u c e", u=2, e=2),
                in0=yb[i].rearrange("p (c u e) -> p u c e", u=2, e=2),
                in1=held["fit", i][:].rearrange("p (c u e) -> p u c e", u=2, e=2),
                op=ALU.subtract,
            )
            held["err", i] = err

        def square(i):
            sq = work.tile([LANES, P], F32)
            nc.scalar.activation(out=sq[:], in_=held["err", i][:], func=ACT.Square)
            held["sq", i] = sq

        def inverse_root(i):
            inv_root = work.tile([LANES, P], F32)
            nc.scalar.activation(out=inv_root[:], in_=held["sq", i][:], func=ACT.Abs_reciprocal_sqrt, scale=16.0, bias=0.16)
            held["inv_root", i] = inv_root

        def fourth_root(i):
            fourth = work.tile([LANES, P], F32)
            nc.scalar.activation(out=fourth[:], in_=held["inv_root", i][:], func=ACT.Abs_reciprocal_sqrt, scale=0.25)
            held["fourth", i] = fourth

        def smooth_sign(i):
            sgn = work.tile([LANES, P], F32)
            nc.vector.tensor_tensor(out=sgn[:], in0=held["err", i][:], in1=held["inv_root", i][:], op=ALU.mult)
            held["sgn", i] = sgn

        def root_sign(i):
            m = work.tile([LANES, P], F32)
            nc.vector.tensor_tensor(
                out=m[:].rearrange("p (u e c) -> p u e c", u=2, e=2),
                in0=held["sgn", i][:].rearrange("p (u c e) -> p u e c", u=2, e=2),
                in1=held["fourth", i][:].rearrange("p (u c e) -> p u e c", u=2, e=2),
                op=ALU.mult,
            )
            held["m", i] = m

        def update_v(i):
            vnew = work.tile([LANES, P], F32)
            nc.vector.tensor_tensor(
                out=vnew[:].rearrange("p (c u e) -> p c u e", u=2, e=2),
                in0=held["sgn", i][:].rearrange("p (u c e) -> p c u e", u=2, e=2),
                in1=vb[i].rearrange("p (c u e) -> p c u e", u=2, e=2),
                op=ALU.add,
            )
            nc.sync.dma_start(out=out_1[i * LANES : (i + 1) * LANES, :], in_=vnew[:])

        def turn_v(i, t):
            if t == 0:
                held["sum", i] = psum.tile([LANES, 4, LANES], F32, name="turned_sum", bufs=1)
            nc.tensor.matmul(held["sum", i][:, t, :], lhsT=vb[i][:, t:P:4], rhs=ident_bf16[:], start=(t == 0), stop=False)

        def turn_m(i):
            for t in range(4):
                nc.tensor.matmul(
                    held["sum", i][:, t, :],
                    lhsT=held["m", i][:, t * LANES : (t + 1) * LANES],
                    rhs=ident[:],
                    is_transpose=True,
                    start=False,
                    stop=(t == 3),
                )

        def apply_gain(i):
            inject = work.tile([LANES, P], BF16, align_bytes=64)
            nc.vector.tensor_tensor(
                out=inject[:].rearrange("p (r i t) -> p r t i", i=2, t=4),
                in0=held["sum", i][:].rearrange("p t (r i) -> p r t i", i=2),
                in1=gain[:].unsqueeze(1).unsqueeze(3).to_broadcast([LANES, LANES // 2, 4, 2]),
                op=ALU.mult,
            )
            held["inject", i] = inject

        def quantise_j(i):
            j_codes = work.tile([LANES, LANES], U32, align_bytes=64)
            j_plane = work.tile([LANES, LANES], U8, align_bytes=64)
            nc.vector.quantize_mx(out=j_codes[:].bitcast(FP8X4), scales=j_plane[:], in_=held["inject", i][:])
            held["jq", i] = (j_codes, j_plane)

        def state_passes(i):
            for h in range(2):
                acc = psum.tile([LANES, BANK], F32, bufs=4)
                for g in range(2):
                    tok = slice(g * LANES, (g + 1) * LANES)
                    codes = a_codes[:, g * N + h * BANK : g * N + (h + 1) * BANK]
                    plane = a_plane[:, g * N + h * BANK : g * N + (h + 1) * BANK]
                    mx(acc[:], held["xq", i], tok, codes, plane, g == 0, False)
                held["acc", i, h] = acc

        def inject_pass(i, h):
            cols = slice(h * BANK, (h + 1) * BANK)
            mx(held["acc", i, h][:], held["jq", i], slice(0, LANES), l_codes[:, cols], l_plane[:, cols], False, True)

        def store_x(i, h):
            xnew = work.tile([LANES, BANK], F32, bufs=4)
            if i == TILES - 1 and h == 1:
                nc.vector.tensor_copy(out=xnew[:], in_=held["acc", i, h][:])
            else:
                nc.scalar.copy(out=xnew[:], in_=held["acc", i, h][:])
            nc.sync.dma_start(out=out_0[i * LANES : (i + 1) * LANES, h * BANK : (h + 1) * BANK], in_=xnew[:])

        def on(stage, i, *rest):
            if 0 <= i < TILES:
                stage(i, *rest)

        def turned_in(s):
            return [s + 4] if 0 <= s + 4 < TILES else []

        for s in range(-5, TILES + 2):
            on(root_sign, s - 1)
            on(square, s)
            on(fit_pass, s + 1, 0)
            on(turn_v, s - 1, 0)
            on(fit_pass, s + 1, 1)
            on(turn_v, s - 1, 1)
            on(inject_pass, s - 2, 0)
            on(turn_v, s - 1, 2)
            on(inject_pass, s - 2, 1)
            on(turn_v, s - 1, 3)
            for i in turned_in(s - 1):
                group_x(i)
            on(update_v, s - 1)
            for i in turned_in(s + 1):
                widen_on_vector(i)
            on(inverse_root, s)
            on(store_x, s - 2, 0)
            on(turn_m, s - 1)
            on(error, s + 1)
            on(apply_gain, s - 1)
            on(smooth_sign, s)
            for i in turned_in(s - 1):
                quantise_x(i)
            on(quantise_j, s - 1)
            on(fourth_root, s)
            on(store_x, s - 2, 1)
            for i in turned_in(s + 1):
                widen_on_scalar(i)
            for i in turned_in(s):
                turn_x(i)
            on(state_passes, s - 1)
